import numpy as np
CORES = [3,11,19,27,35]
N = 5
F = 128
def setup_inputs(rng):
    return {"a": rng.standard_normal((N, 128, 128), dtype=np.float32), "w": rng.standard_normal((N, 128, N * F), dtype=np.float32)}
def reference(a, w):
    tot = np.zeros((128, N * F))
    for j in range(N):
        tot += a[j].astype(np.float64).T @ w[j].astype(np.float64)
    return {"y": np.stack([tot[:, F * r:F * r + F] for r in range(N)]).astype(np.float32 if a.dtype != np.float64 else np.float64)}

@@ -1,0 +1,70 @@
+from concourse.mybir import AluOpType
+
+F = 128
+SCHED = [
+    [3, 2, 0, 4, 1],
+    [2, 4, 1, 0, 3],
+    [1, 3, 4, 2, 0],
+    [4, 0, 3, 1, 2],
+]
+
+SCRATCH = {
+    "aS": ("sbuf", [128, F], "float32"),
+    "wS": ("sbuf", [128, 5 * F], "float32"),
+    "sS": ("sbuf", [128, 4 * F], "float32"),
+    "land": ("sbuf", [128, 4 * F], "float32"),
+    "yS": ("sbuf", [128, F], "float32"),
+    "p0": ("psum", [128, 512], "float32"),
+    "p1": ("psum", [128, 512], "float32"),
+    "p2": ("psum", [128, 512], "float32"),
+    "p3": ("psum", [128, 512], "float32"),
+    "p4": ("psum", [128, 512], "float32"),
+    "p5": ("psum", [128, 512], "float32"),
+}
+SEMAPHORES = (["la", "sent", "st"] + ["lw%d" % k for k in range(5)] + ["mm%d" % k for k in range(5)]
+              + ["cp%d" % k for k in range(4)] + ["arr%d" % k for k in range(4)] + ["ad%d" % k for k in range(4)])
+
+
+def rank_program(g, core, T, topo):
+    r = T.rank_of(core)
+    if r is None:
+        return
+    S = T.sem
+    dests = [SCHED[k][r] for k in range(4)]
+    blocks = dests + [r]
+
+    def sl(k):
+        return slice(k * F, (k + 1) * F)
+
+    g.sync.dma_start(T.aS[:], T.a[:]).then_inc(S.la, 16)
+    for k in range(5):
+        q = g.scalar if k % 2 == 0 else g.sync
+        q.dma_start(T.wS[:, sl(k)], T.w[:, sl(blocks[k])]).then_inc(S["lw%d" % k], 16)
+
+    g.tensor.wait_ge(S.la, 16)
+    for k in range(5):
+        g.tensor.wait_ge(S["lw%d" % k], 16)
+        g.tensor.matmul(T["p%d" % k][:, 0:F], T.aS[:], T.wS[:, sl(k)], True, True).then_inc(S["mm%d" % k], 1)
+
+    for k in range(4):
+        g.vector.wait_ge(S["mm%d" % k], 1)
+        g.vector.tensor_copy(T.sS[:, sl(k)], T["p%d" % k][:, 0:F]).then_inc(S["cp%d" % k], 1)
+
+    for k in range(4):
+        dst = T.cores[dests[k]]
+        rid, pid, _ = topo.addr(dst)
+        g.wait_ge(S["cp%d" % k], 1)
+        g.remote_dma(T.land[:, sl(k)], T.sS[:, sl(k)], S["arr%d" % k], S.sent, pid, rid, 0x00FF)
+
+    g.vector.wait_ge(S.mm4, 1)
+    acc = [T.p4[:, 0:F], T.p5[:, 0:F], T.p4[:, 0:F], T.p5[:, 0:F], T.yS[:]]
+    for k in range(4):
+        g.vector.wait_ge(S["arr%d" % k], 8)
+        if k:
+            g.vector.wait_ge(S["ad%d" % (k - 1)], 1)
+        g.vector.tensor_tensor(acc[k + 1], acc[k], T.land[:, sl(k)], AluOpType.add).then_inc(S["ad%d" % k], 1)
+
+    g.sync.wait_ge(S.ad3, 1)
+    g.sync.dma_start(T.y[:], T.yS[:]).then_inc(S.st, 16)
+    g.sync.wait_ge(S.st, 16)
+    g.wait_ge(S.sent, 32)

@@ -1,11 +1,12 @@
 from concourse.mybir import AluOpType
 
 F = 128
+N = 5
 SCHED = [
-    [3, 2, 0, 4, 1],
-    [2, 4, 1, 0, 3],
-    [1, 3, 4, 2, 0],
-    [4, 0, 3, 1, 2],
+    [3, 2, 3, 4, 1],
+    [1, 4, 1, 0, 3],
+    [2, 0, 4, 2, 0],
+    [4, 3, 0, 1, 2],
 ]
 
 SCRATCH = {
@@ -25,6 +26,20 @@ SEMAPHORES = (["la", "sent", "st"] + ["lw%d" % k for k in range(5)] + ["mm%d" % 
               + ["cp%d" % k for k in range(4)] + ["arr%d" % k for k in range(4)] + ["ad%d" % k for k in range(4)])
 
 
+def sl(k):
+    return slice(k * F, (k + 1) * F)
+
+
+def slot(dst, src):
+    return src if src < dst else src - 1
+
+
+def due(dst, src):
+    k = [SCHED[i][src] for i in range(4)].index(dst)
+    two = (src & 1) != (dst & 1) and (src ^ 1) != dst
+    return k + (1.5 if two else 0.0)
+
+
 def rank_program(g, core, T, topo):
     r = T.rank_of(core)
     if r is None:
@@ -32,9 +47,6 @@ def rank_program(g, core, T, topo):
     S = T.sem
     dests = [SCHED[k][r] for k in range(4)]
     blocks = dests + [r]
-
-    def sl(k):
-        return slice(k * F, (k + 1) * F)
 
     g.sync.dma_start(T.aS[:], T.a[:]).then_inc(S.la, 16)
     for k in range(5):
@@ -51,18 +63,21 @@ def rank_program(g, core, T, topo):
         g.vector.tensor_copy(T.sS[:, sl(k)], T["p%d" % k][:, 0:F]).then_inc(S["cp%d" % k], 1)
 
     for k in range(4):
-        dst = T.cores[dests[k]]
-        rid, pid, _ = topo.addr(dst)
+        d = dests[k]
+        rid, pid, _ = topo.addr(T.cores[d])
+        s = slot(d, r)
         g.wait_ge(S["cp%d" % k], 1)
-        g.remote_dma(T.land[:, sl(k)], T.sS[:, sl(k)], S["arr%d" % k], S.sent, pid, rid, 0x00FF)
+        g.remote_dma(T.land[:, sl(s)], T.sS[:, sl(k)], S["arr%d" % s], S.sent, pid, rid, 0x00FF)
 
+    senders = sorted([j for j in range(N) if j != r], key=lambda j: (due(r, j), j))
     g.vector.wait_ge(S.mm4, 1)
     acc = [T.p4[:, 0:F], T.p5[:, 0:F], T.p4[:, 0:F], T.p5[:, 0:F], T.yS[:]]
-    for k in range(4):
-        g.vector.wait_ge(S["arr%d" % k], 8)
-        if k:
-            g.vector.wait_ge(S["ad%d" % (k - 1)], 1)
-        g.vector.tensor_tensor(acc[k + 1], acc[k], T.land[:, sl(k)], AluOpType.add).then_inc(S["ad%d" % k], 1)
+    for i in range(4):
+        s = slot(r, senders[i])
+        g.vector.wait_ge(S["arr%d" % s], 8)
+        if i:
+            g.vector.wait_ge(S["ad%d" % (i - 1)], 1)
+        g.vector.tensor_tensor(acc[i + 1], acc[i], T.land[:, sl(s)], AluOpType.add).then_inc(S["ad%d" % i], 1)
 
     g.sync.wait_ge(S.ad3, 1)
     g.sync.dma_start(T.y[:], T.yS[:]).then_inc(S.st, 16)

from concourse.mybir import AluOpType

F = 128
N = 5
SCHED = [
    [3, 2, 3, 4, 1],
    [1, 4, 1, 0, 3],
    [2, 0, 4, 2, 0],
    [4, 3, 0, 1, 2],
]

SCRATCH = {
    "aS": ("sbuf", [128, F], "float32"),
    "wS": ("sbuf", [128, 5 * F], "float32"),
    "sS": ("sbuf", [128, 4 * F], "float32"),
    "land": ("sbuf", [128, 4 * F], "float32"),
    "yS": ("sbuf", [128, F], "float32"),
    "p0": ("psum", [128, 512], "float32"),
    "p1": ("psum", [128, 512], "float32"),
    "p2": ("psum", [128, 512], "float32"),
    "p3": ("psum", [128, 512], "float32"),
    "p4": ("psum", [128, 512], "float32"),
    "p5": ("psum", [128, 512], "float32"),
}
SEMAPHORES = (["la", "sent", "st"] + ["lw%d" % k for k in range(5)] + ["mm%d" % k for k in range(5)]
              + ["cp%d" % k for k in range(4)] + ["arr%d" % k for k in range(4)] + ["ad%d" % k for k in range(4)])


def sl(k):
    return slice(k * F, (k + 1) * F)


def slot(dst, src):
    return src if src < dst else src - 1


def due(dst, src):
    k = [SCHED[i][src] for i in range(4)].index(dst)
    two = (src & 1) != (dst & 1) and (src ^ 1) != dst
    return k + (1.5 if two else 0.0)


def rank_program(g, core, T, topo):
    r = T.rank_of(core)
    if r is None:
        return
    S = T.sem
    dests = [SCHED[k][r] for k in range(4)]
    blocks = dests + [r]

    g.sync.dma_start(T.aS[:], T.a[:]).then_inc(S.la, 16)
    for k in range(5):
        q = g.scalar if k % 2 == 0 else g.sync
        q.dma_start(T.wS[:, sl(k)], T.w[:, sl(blocks[k])]).then_inc(S["lw%d" % k], 16)

    g.tensor.wait_ge(S.la, 16)
    for k in range(5):
        g.tensor.wait_ge(S["lw%d" % k], 16)
        g.tensor.matmul(T["p%d" % k][:, 0:F], T.aS[:], T.wS[:, sl(k)], True, True).then_inc(S["mm%d" % k], 1)

    for k in range(4):
        g.vector.wait_ge(S["mm%d" % k], 1)
        g.vector.tensor_copy(T.sS[:, sl(k)], T["p%d" % k][:, 0:F]).then_inc(S["cp%d" % k], 1)

    for k in range(4):
        d = dests[k]
        rid, pid, _ = topo.addr(T.cores[d])
        s = slot(d, r)
        g.wait_ge(S["cp%d" % k], 1)
        g.remote_dma(T.land[:, sl(s)], T.sS[:, sl(k)], S["arr%d" % s], S.sent, pid, rid, 0x00FF)

    senders = sorted([j for j in range(N) if j != r], key=lambda j: (due(r, j), j))
    g.vector.wait_ge(S.mm4, 1)
    acc = [T.p4[:, 0:F], T.p5[:, 0:F], T.p4[:, 0:F], T.p5[:, 0:F], T.yS[:]]
    for i in range(4):
        s = slot(r, senders[i])
        g.vector.wait_ge(S["arr%d" % s], 8)
        if i:
            g.vector.wait_ge(S["ad%d" % (i - 1)], 1)
        g.vector.tensor_tensor(acc[i + 1], acc[i], T.land[:, sl(s)], AluOpType.add).then_inc(S["ad%d" % i], 1)

    g.sync.wait_ge(S.ad3, 1)
    g.sync.dma_start(T.y[:], T.yS[:]).then_inc(S.st, 16)
    g.sync.wait_ge(S.st, 16)
    g.wait_ge(S.sent, 32)
